import numpy as np
import ml_dtypes


def mxq(x, axis, fmt="e4m3"):
    dtype, down = {"e4m3": (ml_dtypes.float8_e4m3fn, 7), "e5m2": (ml_dtypes.float8_e5m2, 14)}[fmt]
    v = np.moveaxis(np.asarray(x, np.float32).astype(ml_dtypes.bfloat16).astype(np.float64), axis, -1)
    blocks = v.reshape(v.shape[:-1] + (-1, 32))
    amax = np.abs(blocks).max(-1, keepdims=True)
    byte = np.maximum(np.where(amax > 0, np.frexp(amax)[1] - 1 + 127, 0) - down, 1)
    scale = np.exp2(byte - 127.0)
    codes = (blocks / scale).astype(np.float32).astype(dtype).astype(np.float64)
    return np.moveaxis((codes * scale).reshape(v.shape), -1, axis)


WIDE = False


def mx_kscale(k):
    if not WIDE:
        return np.ones(k)
    levels = np.array([24, -24, 12, -12, 0])
    if k % 512:
        return np.exp2(np.random.permutation(np.resize(levels, k // 32))).repeat(32)
    a = np.empty((k // 512, 16))
    for p in range(k // 512):
        a[p, :8] = np.random.permutation(np.resize(levels, 8))
        for g in range(8):
            far = levels[np.abs(levels - a[p, g]) >= 10]
            a[p, g + 8] = far[np.random.randint(len(far))]
    return np.exp2(a.ravel()).repeat(32)


def f64(x):
    return np.asarray(x).astype(np.float64)


def striped(idx):
    return np.tile(idx.reshape(-1, 16).T, (8, 1)).astype(np.uint16)


def unstriped(offs):
    return offs[:16].T.reshape(-1).astype(np.int64)


E2M1 = np.array([0.0, 0.5, 1.0, 1.5, 2.0, 3.0, 4.0, 6.0, -0.0, -0.5, -1.0, -1.5, -2.0, -3.0, -4.0, -6.0])


def pack_weight(w, fmt):
    k, n = w.shape
    w = f64(np.asarray(w, np.float32).astype(ml_dtypes.bfloat16)).reshape(k // 32, 32, n)
    amax = np.abs(w).max(1)
    if fmt == "e4m3":
        byte = np.frexp(amax)[1] - 1 + 127 - 7
    else:
        mant, ex = np.frexp(amax / 6.0)
        byte = np.where(mant > 0.5, ex, ex - 1) + 127
    byte = np.clip(np.where(amax > 0, byte, 1), 1, 254)
    scaled = (w * np.exp2(127.0 - byte)[:, None, :]).reshape(k, n).astype(np.float32)
    by_word = np.ascontiguousarray(scaled.reshape(k // 512, 128, 4, n).transpose(0, 1, 3, 2))
    if fmt == "e4m3":
        words = by_word.astype(ml_dtypes.float8_e4m3fn).view(np.uint8)
    else:
        c = by_word.astype(ml_dtypes.float4_e2m1fn).view(np.uint8) & 0xF
        words = (c[..., 0::2] | (c[..., 1::2] << 4)).reshape(k // 512, 128, 2 * n)
    return np.ascontiguousarray(words), np.ascontiguousarray(byte.astype(np.uint8).reshape(k // 512, 16, n))


def unpack_weight(words, scales, fmt):
    g, _, n = scales.shape
    words = np.ascontiguousarray(words).reshape(g, 128, n, -1)
    if fmt == "e4m3":
        vals = words.view(ml_dtypes.float8_e4m3fn).astype(np.float64)
    else:
        nib = np.empty((g, 128, n, 4), np.uint8)
        nib[..., 0::2] = words & 0xF
        nib[..., 1::2] = words >> 4
        vals = E2M1[nib]
    vals = vals * np.repeat(np.exp2(scales.astype(np.float64) - 127.0), 8, axis=1)[..., None]
    return vals.transpose(0, 1, 3, 2).reshape(g * 512, n)


def split(x):
    m, e = np.frexp(f64(x))
    hi = np.ldexp(np.trunc(16.0 * m) / 16.0, e)
    return hi, f64(x) - hi


K, N, T, J = 512, 256, 4096, 2048


def setup_inputs():
    n = np.random.standard_normal
    s = mx_kscale(K)[:, None]
    p_tab = pack_weight(n((K, T)) * s, "e4m3")
    p_tab2 = pack_weight(n((K, T)) * s, "e4m3")
    return {
        "tab_words": p_tab[0],
        "tab_scales": p_tab[1],
        "tab2_words": p_tab2[0],
        "tab2_scales": p_tab2[1],
        "wr": (n((K, N)) / np.sqrt(2 * K) / s).astype(np.float32),
        "wi": (n((K, N)) / np.sqrt(2 * K) / s).astype(np.float32),
        "offs": striped(np.random.permutation(T)[:J]),
    }


def reference(tab_words, tab_scales, tab2_words, tab2_scales, wr, wi, offs):
    idx = unstriped(offs)
    tab_ = unpack_weight(tab_words, tab_scales, "e4m3")[:, idx]
    tab2_ = unpack_weight(tab2_words, tab2_scales, "e4m3")[:, idx]
    wr_hi, wr_lo = split(wr)
    wr_hi_, wr_lo_ = mxq(wr_hi, 0, "e4m3"), mxq(wr_lo, 0, "e4m3")
    wi_ = mxq(f64(wi), 0, "e4m3")
    rr = wr_hi_.T @ tab_ + wr_lo_.T @ tab_
    ii = wi_.T @ tab2_
    zr = rr - ii
    ri = wr_hi_.T @ tab2_ + wr_lo_.T @ tab2_ + wi_.T @ tab_
    zi = ri
    return np.sqrt((zr) ** 2 + (zi) ** 2)

@@ -1,0 +1,144 @@
+from contextlib import ExitStack
+
+import concourse.mybir as mybir
+
+K, N, T, J = 512, 256, 4096, 2048
+FLOPS = 6 * 2 * K * N * J
+
+F32 = mybir.dt.float32
+BF16 = mybir.dt.bfloat16
+I32 = mybir.dt.int32
+U32 = mybir.dt.uint32
+U16 = mybir.dt.uint16
+U8 = mybir.dt.uint8
+FP8X4 = mybir.dt.float8_e4m3fn_x4
+ACT = mybir.ActivationFunctionType
+ALU = mybir.AluOpType
+
+P = 128
+PACK = 4
+CHUNK = 512
+CHUNKS = J // CHUNK
+HALVES = N // P
+HI_MASK = -(1 << 20)
+SCALE_ROW = (0, 4)
+
+
+def tile_list_cpxtab_hl_mag_kernel(
+    tc, tab_words, tab_scales, tab2_words, tab2_scales, wr, wi, offs, out
+):
+    nc = tc.nc
+    with ExitStack() as ctx:
+        keep = ctx.enter_context(tc.tile_pool(name="keep", bufs=1))
+        work = ctx.enter_context(tc.tile_pool(name="work", bufs=4))
+        ring = ctx.enter_context(tc.tile_pool(name="ring", bufs=2))
+        psum = ctx.enter_context(tc.psum_pool(name="psum", bufs=2))
+
+        offsets = keep.tile([P, J // 16], U16, name="offsets")
+        wr_raw = keep.tile([P, PACK, N], F32, name="wr_raw")
+        wi_raw = keep.tile([P, PACK, N], F32, name="wi_raw")
+        scales = [keep.tile([P, T // 4], I32, name="scales%d" % t, align_bytes=64) for t in range(2)]
+        zero = keep.tile([P, 1], F32, name="zero", tag="table0", align_bytes=64)
+        mask = keep.tile([P, 1], I32, name="mask", tag="table1", align_bytes=64)
+        zero_bias = keep.tile([P, 1], F32, name="zero_bias")
+
+        for t in range(2):
+            nc.vector.memset(scales[t][:], 0)
+        nc.gpsimd.memset(zero[:], 0.0)
+        nc.gpsimd.memset(mask[:], HI_MASK)
+        nc.scalar.activation(zero_bias[:], zero[:], ACT.Sqrt)
+
+        nc.sync.dma_start(out=wr_raw[:], in_=wr.rearrange("(p j) n -> p j n", j=PACK))
+        nc.sync.dma_start(offsets[:], offs)
+        for t, (queue, src) in enumerate(((nc.sync, tab_scales), (nc.scalar, tab2_scales))):
+            rows = src[0].bitcast(I32)
+            for r in range(4):
+                queue.dma_start(out=scales[t][SCALE_ROW[t] + r : P : 32, :], in_=rows[r:16:4, :])
+        nc.sync.dma_start(out=wi_raw[:], in_=wi.rearrange("(p j) n -> p j n", j=PACK))
+        names = ("hi", "lo", "wi", "neg_wi")
+        hi32 = keep.tile([P, N, PACK], F32, name="hi32")
+        w16 = {k: keep.tile([P, N, PACK], BF16, name=k + "_bf16", align_bytes=64) for k in names}
+        w_codes = {k: keep.tile([P, N], U32, name=k + "_codes", align_bytes=64) for k in names}
+        w_scales = {k: keep.tile([P, N], U8, name=k + "_scales", align_bytes=64) for k in names}
+        wr_by_n = wr_raw[:].rearrange("p j n -> p n j")
+        wi_by_n = wi_raw[:].rearrange("p j n -> p n j")
+        nc.vector.tensor_scalar(
+            out=hi32[:].bitcast(I32),
+            in0=wr_raw[:].bitcast(I32).rearrange("p j n -> p n j"),
+            scalar1=mask[:],
+            scalar2=None,
+            op0=ALU.bitwise_and,
+        )
+        words = [keep.tile([P, T], I32, name="words%d" % t, tag="table%d" % t, align_bytes=64) for t in range(2)]
+        for t, src in enumerate((tab_words, tab2_words)):
+            nc.sync.dma_start(out=words[t][:], in_=src[0].rearrange("p t i -> p (t i)").bitcast(I32))
+        nc.scalar.activation(w16["hi"][:], hi32[:], ACT.Copy)
+        nc.vector.tensor_tensor(out=w16["lo"][:], in0=wr_by_n, in1=hi32[:], op=ALU.subtract)
+        nc.scalar.activation(w16["wi"][:], wi_by_n, ACT.Copy)
+        nc.scalar.activation(w16["neg_wi"][:], wi_by_n, ACT.Copy, scale=-1.0)
+
+        def quantise(k):
+            nc.vector.quantize_mx(
+                out=w_codes[k][:].bitcast(FP8X4),
+                scales=w_scales[k][:],
+                in_=w16[k][:].rearrange("p n j -> p (n j)"),
+            )
+
+        def gather(c, t):
+            entries = offsets[:, c * CHUNK // 16 : (c + 1) * CHUNK // 16]
+            g_scales = ring.tile([P, CHUNK], U8, name="g_scales%d" % t, align_bytes=64)
+            g_words = ring.tile([P, CHUNK], U32, name="g_words%d" % t, align_bytes=64)
+            nc.vector.tensor_copy(g_scales[:], scales[t][:].bitcast(U8).indirect(entries))
+            nc.vector.tensor_copy(g_words[:], words[t][:].bitcast(U32).indirect(entries))
+            return g_words, g_scales
+
+        def mx_pass(acc, k, h, gathered, t, start, stop):
+            cols = slice(h * P, (h + 1) * P)
+            g_words, g_scales = gathered
+            nc.tensor.matmul_mx(
+                out=acc[:],
+                lhsT=w_codes[k][:, cols].bitcast(FP8X4),
+                lhsT_scale=w_scales[k][:, cols],
+                rhs=g_words[:].bitcast(FP8X4),
+                rhs_scale=g_scales[SCALE_ROW[t] : P, :],
+                start=start,
+                stop=stop,
+            )
+
+        def finish(c, h, total):
+            result = work.tile([P, CHUNK], F32, name="result")
+            nc.scalar.activation(result[:], total[:], ACT.Sqrt)
+            nc.sync.dma_start(out=out[h * P : (h + 1) * P, c * CHUNK : (c + 1) * CHUNK], in_=result[:])
+
+        pending = []
+        for c in range(CHUNKS):
+            v = gather(c, 0)
+            if c == 0:
+                for k in names:
+                    quantise(k)
+            v2 = gather(c, 1)
+            zr = [psum.tile([P, CHUNK], F32, name="zr%d" % h) for h in range(HALVES)]
+            zi = [psum.tile([P, CHUNK], F32, name="zi%d" % h) for h in range(HALVES)]
+            for h in range(HALVES):
+                mx_pass(zr[h], "hi", h, v, 0, True, False)
+                mx_pass(zr[h], "lo", h, v, 0, False, False)
+            mx_pass(zi[1], "wi", 1, v, 0, True, False)
+            mx_pass(zr[0], "neg_wi", 0, v2, 1, False, True)
+            mx_pass(zi[0], "hi", 0, v2, 1, True, False)
+            mx_pass(zi[0], "wi", 0, v, 0, False, False)
+            mx_pass(zi[0], "lo", 0, v2, 1, False, True)
+            mx_pass(zr[1], "neg_wi", 1, v2, 1, False, True)
+            mx_pass(zi[1], "hi", 1, v2, 1, False, False)
+            mx_pass(zi[1], "lo", 1, v2, 1, False, True)
+            for h in range(HALVES):
+                zr_sq = work.tile([P, CHUNK], F32, name="zr_sq")
+                zi_sq = work.tile([P, CHUNK], F32, name="zi_sq")
+                total = work.tile([P, CHUNK], F32, name="total")
+                nc.scalar.activation(zr_sq[:], zr[h][:], ACT.Square, bias=zero_bias[:])
+                nc.scalar.activation(zi_sq[:], zi[h][:], ACT.Square, bias=zero_bias[:])
+                adder = nc.vector if c == CHUNKS - 1 else nc.gpsimd
+                adder.tensor_tensor(out=total[:], in0=zr_sq[:], in1=zi_sq[:], op=ALU.add)
+                if pending:
+                    finish(*pending[-1])
+                pending.append((c, h, total))
+        finish(*pending[-1])

@@ -22,6 +22,7 @@ CHUNKS = J // CHUNK
 HALVES = N // P
 HI_MASK = -(1 << 20)
 SCALE_ROW = (0, 4)
+SQRT_LAG = 3
 
 
 def tile_list_cpxtab_hl_mag_kernel(
@@ -30,23 +31,26 @@ def tile_list_cpxtab_hl_mag_kernel(
     nc = tc.nc
     with ExitStack() as ctx:
         keep = ctx.enter_context(tc.tile_pool(name="keep", bufs=1))
-        work = ctx.enter_context(tc.tile_pool(name="work", bufs=4))
+        work = ctx.enter_context(tc.tile_pool(name="work", bufs=8))
         ring = ctx.enter_context(tc.tile_pool(name="ring", bufs=2))
+        loads = ctx.enter_context(tc.tile_pool(name="loads", bufs=1))
         psum = ctx.enter_context(tc.psum_pool(name="psum", bufs=2))
 
         offsets = keep.tile([P, J // 16], U16, name="offsets")
         wr_raw = keep.tile([P, PACK, N], F32, name="wr_raw")
-        wi_raw = keep.tile([P, PACK, N], F32, name="wi_raw")
         scales = [keep.tile([P, T // 4], I32, name="scales%d" % t, align_bytes=64) for t in range(2)]
-        zero = keep.tile([P, 1], F32, name="zero", tag="table0", align_bytes=64)
-        mask = keep.tile([P, 1], I32, name="mask", tag="table1", align_bytes=64)
+        zero = loads.tile([P, PACK * N + 2 * T], F32, name="zero", offset=0)
+        wi_raw = loads.tile([P, PACK, N], F32, name="wi_raw", offset=0)
+        words = [
+            loads.tile([P, T], I32, name="words%d" % t, offset=4 * (PACK * N + t * T), align_bytes=64)
+            for t in range(2)
+        ]
         zero_bias = keep.tile([P, 1], F32, name="zero_bias")
 
         for t in range(2):
             nc.vector.memset(scales[t][:], 0)
-        nc.gpsimd.memset(zero[:], 0.0)
-        nc.gpsimd.memset(mask[:], HI_MASK)
-        nc.scalar.activation(zero_bias[:], zero[:], ACT.Sqrt)
+        nc.gpsimd.memset(zero[:, 0:1], 0.0)
+        nc.scalar.activation(zero_bias[:], zero[:, 0:1], ACT.Sqrt)
 
         nc.sync.dma_start(out=wr_raw[:], in_=wr.rearrange("(p j) n -> p j n", j=PACK))
         nc.sync.dma_start(offsets[:], offs)
@@ -55,6 +59,9 @@ def tile_list_cpxtab_hl_mag_kernel(
             for r in range(4):
                 queue.dma_start(out=scales[t][SCALE_ROW[t] + r : P : 32, :], in_=rows[r:16:4, :])
         nc.sync.dma_start(out=wi_raw[:], in_=wi.rearrange("(p j) n -> p j n", j=PACK))
+        for t, src in enumerate((tab_words, tab2_words)):
+            nc.sync.dma_start(out=words[t][:], in_=src[0].rearrange("p t i -> p (t i)").bitcast(I32))
+
         names = ("hi", "lo", "wi", "neg_wi")
         hi32 = keep.tile([P, N, PACK], F32, name="hi32")
         w16 = {k: keep.tile([P, N, PACK], BF16, name=k + "_bf16", align_bytes=64) for k in names}
@@ -65,13 +72,10 @@ def tile_list_cpxtab_hl_mag_kernel(
         nc.vector.tensor_scalar(
             out=hi32[:].bitcast(I32),
             in0=wr_raw[:].bitcast(I32).rearrange("p j n -> p n j"),
-            scalar1=mask[:],
+            scalar1=HI_MASK,
             scalar2=None,
             op0=ALU.bitwise_and,
         )
-        words = [keep.tile([P, T], I32, name="words%d" % t, tag="table%d" % t, align_bytes=64) for t in range(2)]
-        for t, src in enumerate((tab_words, tab2_words)):
-            nc.sync.dma_start(out=words[t][:], in_=src[0].rearrange("p t i -> p (t i)").bitcast(I32))
         nc.scalar.activation(w16["hi"][:], hi32[:], ACT.Copy)
         nc.vector.tensor_tensor(out=w16["lo"][:], in0=wr_by_n, in1=hi32[:], op=ALU.subtract)
         nc.scalar.activation(w16["wi"][:], wi_by_n, ACT.Copy)
@@ -87,7 +91,7 @@ def tile_list_cpxtab_hl_mag_kernel(
         def gather(c, t):
             entries = offsets[:, c * CHUNK // 16 : (c + 1) * CHUNK // 16]
             g_scales = ring.tile([P, CHUNK], U8, name="g_scales%d" % t, align_bytes=64)
-            g_words = ring.tile([P, CHUNK], U32, name="g_words%d" % t, align_bytes=64)
+            g_words = ring.tile([P, CHUNK], U32, name="g_words%d" % t, bufs=3 - t, align_bytes=64)
             nc.vector.tensor_copy(g_scales[:], scales[t][:].bitcast(U8).indirect(entries))
             nc.vector.tensor_copy(g_words[:], words[t][:].bitcast(U32).indirect(entries))
             return g_words, g_scales
@@ -136,9 +140,9 @@ def tile_list_cpxtab_hl_mag_kernel(
                 total = work.tile([P, CHUNK], F32, name="total")
                 nc.scalar.activation(zr_sq[:], zr[h][:], ACT.Square, bias=zero_bias[:])
                 nc.scalar.activation(zi_sq[:], zi[h][:], ACT.Square, bias=zero_bias[:])
-                adder = nc.vector if c == CHUNKS - 1 else nc.gpsimd
-                adder.tensor_tensor(out=total[:], in0=zr_sq[:], in1=zi_sq[:], op=ALU.add)
-                if pending:
-                    finish(*pending[-1])
+                nc.vector.tensor_tensor(out=total[:], in0=zr_sq[:], in1=zi_sq[:], op=ALU.add)
                 pending.append((c, h, total))
-        finish(*pending[-1])
+                if len(pending) > SQRT_LAG:
+                    finish(*pending[-1 - SQRT_LAG])
+        for late in pending[-SQRT_LAG:]:
+            finish(*late)

@@ -22,7 +22,7 @@ CHUNKS = J // CHUNK
 HALVES = N // P
 HI_MASK = -(1 << 20)
 SCALE_ROW = (0, 4)
-SQRT_LAG = 3
+SQRT_LAG = 2
 
 
 def tile_list_cpxtab_hl_mag_kernel(
@@ -54,7 +54,7 @@ def tile_list_cpxtab_hl_mag_kernel(
 
         nc.sync.dma_start(out=wr_raw[:], in_=wr.rearrange("(p j) n -> p j n", j=PACK))
         nc.sync.dma_start(offsets[:], offs)
-        for t, (queue, src) in enumerate(((nc.sync, tab_scales), (nc.scalar, tab2_scales))):
+        for t, (queue, src) in enumerate(((nc.sync, tab_scales), (nc.gpsimd, tab2_scales))):
             rows = src[0].bitcast(I32)
             for r in range(4):
                 queue.dma_start(out=scales[t][SCALE_ROW[t] + r : P : 32, :], in_=rows[r:16:4, :])
@@ -64,7 +64,7 @@ def tile_list_cpxtab_hl_mag_kernel(
 
         names = ("hi", "lo", "wi", "neg_wi")
         hi32 = keep.tile([P, N, PACK], F32, name="hi32")
-        w16 = {k: keep.tile([P, N, PACK], BF16, name=k + "_bf16", align_bytes=64) for k in names}
+        w16 = {k: keep.tile([P, N, PACK], BF16, name=k + "_bf16", tag=k, align_bytes=64) for k in names}
         w_codes = {k: keep.tile([P, N], U32, name=k + "_codes", align_bytes=64) for k in names}
         w_scales = {k: keep.tile([P, N], U8, name=k + "_scales", align_bytes=64) for k in names}
         wr_by_n = wr_raw[:].rearrange("p j n -> p n j")
@@ -77,7 +77,7 @@ def tile_list_cpxtab_hl_mag_kernel(
             op0=ALU.bitwise_and,
         )
         nc.scalar.activation(w16["hi"][:], hi32[:], ACT.Copy)
-        nc.vector.tensor_tensor(out=w16["lo"][:], in0=wr_by_n, in1=hi32[:], op=ALU.subtract)
+        nc.gpsimd.tensor_tensor(out=w16["lo"][:], in0=wr_by_n, in1=hi32[:], op=ALU.subtract)
         nc.scalar.activation(w16["wi"][:], wi_by_n, ACT.Copy)
         nc.scalar.activation(w16["neg_wi"][:], wi_by_n, ACT.Copy, scale=-1.0)
 
@@ -91,7 +91,10 @@ def tile_list_cpxtab_hl_mag_kernel(
         def gather(c, t):
             entries = offsets[:, c * CHUNK // 16 : (c + 1) * CHUNK // 16]
             g_scales = ring.tile([P, CHUNK], U8, name="g_scales%d" % t, align_bytes=64)
-            g_words = ring.tile([P, CHUNK], U32, name="g_words%d" % t, bufs=3 - t, align_bytes=64)
+            if t == 0:
+                g_words = keep.tile([P, CHUNK], U32, name="g_words0", tag=names[c], align_bytes=64)
+            else:
+                g_words = ring.tile([P, CHUNK], U32, name="g_words1", align_bytes=64)
             nc.vector.tensor_copy(g_scales[:], scales[t][:].bitcast(U8).indirect(entries))
             nc.vector.tensor_copy(g_words[:], words[t][:].bitcast(U32).indirect(entries))
             return g_words, g_scales
@@ -109,39 +112,61 @@ def tile_list_cpxtab_hl_mag_kernel(
                 stop=stop,
             )
 
-        def finish(c, h, total):
-            result = work.tile([P, CHUNK], F32, name="result")
-            nc.scalar.activation(result[:], total[:], ACT.Sqrt)
-            nc.sync.dma_start(out=out[h * P : (h + 1) * P, c * CHUNK : (c + 1) * CHUNK], in_=result[:])
+        def finish(h, pieces):
+            for j0, width, total in pieces:
+                result = work.tile([P, width], F32, name="result")
+                nc.scalar.activation(result[:], total[:], ACT.Sqrt)
+                nc.sync.dma_start(out=out[h * P : (h + 1) * P, j0 : j0 + width], in_=result[:])
 
+        for k in names:
+            quantise(k)
         pending = []
         for c in range(CHUNKS):
             v = gather(c, 0)
-            if c == 0:
-                for k in names:
-                    quantise(k)
             v2 = gather(c, 1)
             zr = [psum.tile([P, CHUNK], F32, name="zr%d" % h) for h in range(HALVES)]
             zi = [psum.tile([P, CHUNK], F32, name="zi%d" % h) for h in range(HALVES)]
+            last = c == CHUNKS - 1
             for h in range(HALVES):
                 mx_pass(zr[h], "hi", h, v, 0, True, False)
+            for h in range(HALVES):
                 mx_pass(zr[h], "lo", h, v, 0, False, False)
             mx_pass(zi[1], "wi", 1, v, 0, True, False)
-            mx_pass(zr[0], "neg_wi", 0, v2, 1, False, True)
-            mx_pass(zi[0], "hi", 0, v2, 1, True, False)
-            mx_pass(zi[0], "wi", 0, v, 0, False, False)
-            mx_pass(zi[0], "lo", 0, v2, 1, False, True)
-            mx_pass(zr[1], "neg_wi", 1, v2, 1, False, True)
-            mx_pass(zi[1], "hi", 1, v2, 1, False, False)
-            mx_pass(zi[1], "lo", 1, v2, 1, False, True)
+            if last:
+                mx_pass(zi[0], "wi", 0, v, 0, True, False)
+                for h in range(HALVES):
+                    mx_pass(zr[h], "neg_wi", h, v2, 1, False, True)
+                    mx_pass(zi[h], "hi", h, v2, 1, False, False)
+                    mx_pass(zi[h], "lo", h, v2, 1, False, True)
+            else:
+                mx_pass(zr[0], "neg_wi", 0, v2, 1, False, True)
+                mx_pass(zi[0], "hi", 0, v2, 1, True, False)
+                mx_pass(zi[0], "wi", 0, v, 0, False, False)
+                mx_pass(zi[0], "lo", 0, v2, 1, False, True)
+                mx_pass(zr[1], "neg_wi", 1, v2, 1, False, True)
+                mx_pass(zi[1], "hi", 1, v2, 1, False, False)
+                mx_pass(zi[1], "lo", 1, v2, 1, False, True)
             for h in range(HALVES):
                 zr_sq = work.tile([P, CHUNK], F32, name="zr_sq")
                 zi_sq = work.tile([P, CHUNK], F32, name="zi_sq")
-                total = work.tile([P, CHUNK], F32, name="total")
-                nc.scalar.activation(zr_sq[:], zr[h][:], ACT.Square, bias=zero_bias[:])
+                if last:
+                    zr_copy = ring.tile([P, CHUNK], F32, name="zr_copy")
+                    nc.vector.tensor_copy(zr_copy[:], zr[h][:])
+                    nc.vector.tensor_tensor(out=zr_sq[:], in0=zr[h][:], in1=zr_copy[:], op=ALU.mult)
+                else:
+                    nc.scalar.activation(zr_sq[:], zr[h][:], ACT.Square, bias=zero_bias[:])
                 nc.scalar.activation(zi_sq[:], zi[h][:], ACT.Square, bias=zero_bias[:])
-                nc.vector.tensor_tensor(out=total[:], in0=zr_sq[:], in1=zi_sq[:], op=ALU.add)
-                pending.append((c, h, total))
+                very_last = last and h == HALVES - 1
+                width = CHUNK // 2 if very_last else CHUNK
+                pieces = []
+                for j0 in range(0, CHUNK, width):
+                    total = work.tile([P, width], F32, name="total")
+                    adder = nc.vector if very_last else nc.gpsimd
+                    adder.tensor_tensor(
+                        out=total[:], in0=zr_sq[:, j0 : j0 + width], in1=zi_sq[:, j0 : j0 + width], op=ALU.add
+                    )
+                    pieces.append((c * CHUNK + j0, width, total))
+                pending.append((h, pieces))
                 if len(pending) > SQRT_LAG:
                     finish(*pending[-1 - SQRT_LAG])
         for late in pending[-SQRT_LAG:]:

@@ -49,12 +49,12 @@ def tile_list_cpxtab_hl_mag_kernel(
 
         for t in range(2):
             nc.vector.memset(scales[t][:], 0)
-        nc.gpsimd.memset(zero[:, 0:1], 0.0)
+        nc.vector.memset(zero[:, 0:1], 0.0)
         nc.scalar.activation(zero_bias[:], zero[:, 0:1], ACT.Sqrt)
 
         nc.sync.dma_start(out=wr_raw[:], in_=wr.rearrange("(p j) n -> p j n", j=PACK))
         nc.sync.dma_start(offsets[:], offs)
-        for t, (queue, src) in enumerate(((nc.sync, tab_scales), (nc.gpsimd, tab2_scales))):
+        for t, (queue, src) in enumerate(((nc.sync, tab_scales), (nc.sync, tab2_scales))):
             rows = src[0].bitcast(I32)
             for r in range(4):
                 queue.dma_start(out=scales[t][SCALE_ROW[t] + r : P : 32, :], in_=rows[r:16:4, :])

@@ -17,12 +17,18 @@ ALU = mybir.AluOpType
 
 P = 128
 PACK = 4
+QUADRANT = 32
+SCALE_ROWS = 16
+GROUP = 16
 CHUNK = 512
 CHUNKS = J // CHUNK
 HALVES = N // P
 HI_MASK = -(1 << 20)
 SCALE_ROW = (0, 4)
 SQRT_LAG = 2
+WORK_BUFS = 8
+RING_BUFS = 2
+WORD_SLOTS = 3
 
 
 def tile_list_cpxtab_hl_mag_kernel(
@@ -31,12 +37,12 @@ def tile_list_cpxtab_hl_mag_kernel(
     nc = tc.nc
     with ExitStack() as ctx:
         keep = ctx.enter_context(tc.tile_pool(name="keep", bufs=1))
-        work = ctx.enter_context(tc.tile_pool(name="work", bufs=8))
-        ring = ctx.enter_context(tc.tile_pool(name="ring", bufs=2))
+        work = ctx.enter_context(tc.tile_pool(name="work", bufs=WORK_BUFS))
+        ring = ctx.enter_context(tc.tile_pool(name="ring", bufs=RING_BUFS))
         loads = ctx.enter_context(tc.tile_pool(name="loads", bufs=1))
-        psum = ctx.enter_context(tc.psum_pool(name="psum", bufs=2))
+        psum = ctx.enter_context(tc.psum_pool(name="psum", bufs=RING_BUFS))
 
-        offsets = keep.tile([P, J // 16], U16, name="offsets")
+        offsets = keep.tile([P, J // GROUP], U16, name="offsets")
         wr_raw = keep.tile([P, PACK, N], F32, name="wr_raw")
         scales = [keep.tile([P, T // 4], I32, name="scales%d" % t, align_bytes=64) for t in range(2)]
         zero = loads.tile([P, PACK * N + 2 * T], F32, name="zero", offset=0)
@@ -49,63 +55,64 @@ def tile_list_cpxtab_hl_mag_kernel(
 
         for t in range(2):
             nc.vector.memset(scales[t][:], 0)
-        nc.vector.memset(zero[:, 0:1], 0.0)
+        nc.gpsimd.memset(zero[:, 0:1], 0.0)
         nc.scalar.activation(zero_bias[:], zero[:, 0:1], ACT.Sqrt)
 
         nc.sync.dma_start(out=wr_raw[:], in_=wr.rearrange("(p j) n -> p j n", j=PACK))
         nc.sync.dma_start(offsets[:], offs)
-        for t, (queue, src) in enumerate(((nc.sync, tab_scales), (nc.sync, tab2_scales))):
+        for t, (queue, src) in enumerate(((nc.sync, tab_scales), (nc.scalar, tab2_scales))):
             rows = src[0].bitcast(I32)
             for r in range(4):
-                queue.dma_start(out=scales[t][SCALE_ROW[t] + r : P : 32, :], in_=rows[r:16:4, :])
+                queue.dma_start(out=scales[t][SCALE_ROW[t] + r : P : QUADRANT, :], in_=rows[r:SCALE_ROWS:4, :])
         nc.sync.dma_start(out=wi_raw[:], in_=wi.rearrange("(p j) n -> p j n", j=PACK))
         for t, src in enumerate((tab_words, tab2_words)):
             nc.sync.dma_start(out=words[t][:], in_=src[0].rearrange("p t i -> p (t i)").bitcast(I32))
 
         names = ("hi", "lo", "wi", "neg_wi")
-        hi32 = keep.tile([P, N, PACK], F32, name="hi32")
-        w16 = {k: keep.tile([P, N, PACK], BF16, name=k + "_bf16", tag=k, align_bytes=64) for k in names}
-        w_codes = {k: keep.tile([P, N], U32, name=k + "_codes", align_bytes=64) for k in names}
-        w_scales = {k: keep.tile([P, N], U8, name=k + "_scales", align_bytes=64) for k in names}
-        wr_by_n = wr_raw[:].rearrange("p j n -> p n j")
+        hi32 = keep.tile([P, PACK, N], F32, name="hi32")
+        lo32 = keep.tile([P, PACK, N], F32, name="lo32")
+        w16 = {w: keep.tile([P, N, PACK], BF16, name=w + "_bf16", tag=w, align_bytes=64) for w in names}
+        w_codes = {w: keep.tile([P, N], U32, name=w + "_codes", align_bytes=64) for w in names}
+        w_scales = {w: keep.tile([P, N], U8, name=w + "_scales", align_bytes=64) for w in names}
         wi_by_n = wi_raw[:].rearrange("p j n -> p n j")
         nc.vector.tensor_scalar(
             out=hi32[:].bitcast(I32),
-            in0=wr_raw[:].bitcast(I32).rearrange("p j n -> p n j"),
+            in0=wr_raw[:].bitcast(I32),
             scalar1=HI_MASK,
             scalar2=None,
             op0=ALU.bitwise_and,
         )
-        nc.scalar.activation(w16["hi"][:], hi32[:], ACT.Copy)
-        nc.gpsimd.tensor_tensor(out=w16["lo"][:], in0=wr_by_n, in1=hi32[:], op=ALU.subtract)
+        nc.vector.tensor_tensor(out=lo32[:], in0=wr_raw[:], in1=hi32[:], op=ALU.subtract)
+        nc.scalar.activation(w16["hi"][:], hi32[:].rearrange("p j n -> p n j"), ACT.Copy)
+        nc.scalar.activation(w16["lo"][:], lo32[:].rearrange("p j n -> p n j"), ACT.Copy)
         nc.scalar.activation(w16["wi"][:], wi_by_n, ACT.Copy)
         nc.scalar.activation(w16["neg_wi"][:], wi_by_n, ACT.Copy, scale=-1.0)
 
-        def quantise(k):
+        def quantise(w):
             nc.vector.quantize_mx(
-                out=w_codes[k][:].bitcast(FP8X4),
-                scales=w_scales[k][:],
-                in_=w16[k][:].rearrange("p n j -> p (n j)"),
+                out=w_codes[w][:].bitcast(FP8X4),
+                scales=w_scales[w][:],
+                in_=w16[w][:].rearrange("p n j -> p (n j)"),
             )
 
         def gather(c, t):
-            entries = offsets[:, c * CHUNK // 16 : (c + 1) * CHUNK // 16]
+            entries = offsets[:, c * CHUNK // GROUP : (c + 1) * CHUNK // GROUP]
             g_scales = ring.tile([P, CHUNK], U8, name="g_scales%d" % t, align_bytes=64)
             if t == 0:
-                g_words = keep.tile([P, CHUNK], U32, name="g_words0", tag=names[c], align_bytes=64)
+                g_words = keep.tile([P, CHUNK], U32, name="g_words0", tag=names[c % WORD_SLOTS], align_bytes=64)
             else:
-                g_words = ring.tile([P, CHUNK], U32, name="g_words1", align_bytes=64)
+                g_words = ring.tile([P, CHUNK], U32, name="g_words1", bufs=WORD_SLOTS, align_bytes=64)
             nc.vector.tensor_copy(g_scales[:], scales[t][:].bitcast(U8).indirect(entries))
             nc.vector.tensor_copy(g_words[:], words[t][:].bitcast(U32).indirect(entries))
             return g_words, g_scales
 
-        def mx_pass(acc, k, h, gathered, t, start, stop):
+        def mx_pass(acc, w, h, gathered, t, start, stop):
             cols = slice(h * P, (h + 1) * P)
             g_words, g_scales = gathered
             nc.tensor.matmul_mx(
                 out=acc[:],
-                lhsT=w_codes[k][:, cols].bitcast(FP8X4),
-                lhsT_scale=w_scales[k][:, cols],
+                lhsT=w_codes[w][:, cols].bitcast(FP8X4),
+                lhsT_scale=w_scales[w][:, cols],
                 rhs=g_words[:].bitcast(FP8X4),
                 rhs_scale=g_scales[SCALE_ROW[t] : P, :],
                 start=start,
@@ -118,8 +125,8 @@ def tile_list_cpxtab_hl_mag_kernel(
                 nc.scalar.activation(result[:], total[:], ACT.Sqrt)
                 nc.sync.dma_start(out=out[h * P : (h + 1) * P, j0 : j0 + width], in_=result[:])
 
-        for k in names:
-            quantise(k)
+        for w in names:
+            quantise(w)
         pending = []
         for c in range(CHUNKS):
             v = gather(c, 0)
@@ -131,37 +138,28 @@ def tile_list_cpxtab_hl_mag_kernel(
                 mx_pass(zr[h], "hi", h, v, 0, True, False)
             for h in range(HALVES):
                 mx_pass(zr[h], "lo", h, v, 0, False, False)
-            mx_pass(zi[1], "wi", 1, v, 0, True, False)
+            mx_pass(zi[0], "wi", 0, v, 0, True, False)
             if last:
-                mx_pass(zi[0], "wi", 0, v, 0, True, False)
-                for h in range(HALVES):
-                    mx_pass(zr[h], "neg_wi", h, v2, 1, False, True)
-                    mx_pass(zi[h], "hi", h, v2, 1, False, False)
-                    mx_pass(zi[h], "lo", h, v2, 1, False, True)
-            else:
-                mx_pass(zr[0], "neg_wi", 0, v2, 1, False, True)
-                mx_pass(zi[0], "hi", 0, v2, 1, True, False)
-                mx_pass(zi[0], "wi", 0, v, 0, False, False)
-                mx_pass(zi[0], "lo", 0, v2, 1, False, True)
-                mx_pass(zr[1], "neg_wi", 1, v2, 1, False, True)
-                mx_pass(zi[1], "hi", 1, v2, 1, False, False)
-                mx_pass(zi[1], "lo", 1, v2, 1, False, True)
+                mx_pass(zi[1], "wi", 1, v, 0, True, False)
+            mx_pass(zr[0], "neg_wi", 0, v2, 1, False, True)
+            mx_pass(zi[0], "hi", 0, v2, 1, False, False)
+            mx_pass(zi[0], "lo", 0, v2, 1, False, True)
+            mx_pass(zr[1], "neg_wi", 1, v2, 1, False, True)
+            mx_pass(zi[1], "hi", 1, v2, 1, not last, False)
+            if not last:
+                mx_pass(zi[1], "wi", 1, v, 0, False, False)
+            mx_pass(zi[1], "lo", 1, v2, 1, False, True)
             for h in range(HALVES):
                 zr_sq = work.tile([P, CHUNK], F32, name="zr_sq")
                 zi_sq = work.tile([P, CHUNK], F32, name="zi_sq")
-                if last:
-                    zr_copy = ring.tile([P, CHUNK], F32, name="zr_copy")
-                    nc.vector.tensor_copy(zr_copy[:], zr[h][:])
-                    nc.vector.tensor_tensor(out=zr_sq[:], in0=zr[h][:], in1=zr_copy[:], op=ALU.mult)
-                else:
-                    nc.scalar.activation(zr_sq[:], zr[h][:], ACT.Square, bias=zero_bias[:])
+                nc.scalar.activation(zr_sq[:], zr[h][:], ACT.Square, bias=zero_bias[:])
                 nc.scalar.activation(zi_sq[:], zi[h][:], ACT.Square, bias=zero_bias[:])
                 very_last = last and h == HALVES - 1
                 width = CHUNK // 2 if very_last else CHUNK
                 pieces = []
                 for j0 in range(0, CHUNK, width):
                     total = work.tile([P, width], F32, name="total")
-                    adder = nc.vector if very_last else nc.gpsimd
+                    adder = nc.vector if last else nc.gpsimd
                     adder.tensor_tensor(
                         out=total[:], in0=zr_sq[:, j0 : j0 + width], in1=zi_sq[:, j0 : j0 + width], op=ALU.add
                     )

from contextlib import ExitStack

import concourse.mybir as mybir

K, N, T, J = 512, 256, 4096, 2048
FLOPS = 6 * 2 * K * N * J

F32 = mybir.dt.float32
BF16 = mybir.dt.bfloat16
I32 = mybir.dt.int32
U32 = mybir.dt.uint32
U16 = mybir.dt.uint16
U8 = mybir.dt.uint8
FP8X4 = mybir.dt.float8_e4m3fn_x4
ACT = mybir.ActivationFunctionType
ALU = mybir.AluOpType

P = 128
PACK = 4
QUADRANT = 32
SCALE_ROWS = 16
GROUP = 16
CHUNK = 512
CHUNKS = J // CHUNK
HALVES = N // P
HI_MASK = -(1 << 20)
SCALE_ROW = (0, 4)
SQRT_LAG = 2
WORK_BUFS = 8
RING_BUFS = 2
WORD_SLOTS = 3


def tile_list_cpxtab_hl_mag_kernel(
    tc, tab_words, tab_scales, tab2_words, tab2_scales, wr, wi, offs, out
):
    nc = tc.nc
    with ExitStack() as ctx:
        keep = ctx.enter_context(tc.tile_pool(name="keep", bufs=1))
        work = ctx.enter_context(tc.tile_pool(name="work", bufs=WORK_BUFS))
        ring = ctx.enter_context(tc.tile_pool(name="ring", bufs=RING_BUFS))
        loads = ctx.enter_context(tc.tile_pool(name="loads", bufs=1))
        psum = ctx.enter_context(tc.psum_pool(name="psum", bufs=RING_BUFS))

        offsets = keep.tile([P, J // GROUP], U16, name="offsets")
        wr_raw = keep.tile([P, PACK, N], F32, name="wr_raw")
        scales = [keep.tile([P, T // 4], I32, name="scales%d" % t, align_bytes=64) for t in range(2)]
        zero = loads.tile([P, PACK * N + 2 * T], F32, name="zero", offset=0)
        wi_raw = loads.tile([P, PACK, N], F32, name="wi_raw", offset=0)
        words = [
            loads.tile([P, T], I32, name="words%d" % t, offset=4 * (PACK * N + t * T), align_bytes=64)
            for t in range(2)
        ]
        zero_bias = keep.tile([P, 1], F32, name="zero_bias")

        for t in range(2):
            nc.vector.memset(scales[t][:], 0)
        nc.gpsimd.memset(zero[:, 0:1], 0.0)
        nc.scalar.activation(zero_bias[:], zero[:, 0:1], ACT.Sqrt)

        nc.sync.dma_start(out=wr_raw[:], in_=wr.rearrange("(p j) n -> p j n", j=PACK))
        nc.sync.dma_start(offsets[:], offs)
        for t, (queue, src) in enumerate(((nc.sync, tab_scales), (nc.scalar, tab2_scales))):
            rows = src[0].bitcast(I32)
            for r in range(4):
                queue.dma_start(out=scales[t][SCALE_ROW[t] + r : P : QUADRANT, :], in_=rows[r:SCALE_ROWS:4, :])
        nc.sync.dma_start(out=wi_raw[:], in_=wi.rearrange("(p j) n -> p j n", j=PACK))
        for t, src in enumerate((tab_words, tab2_words)):
            nc.sync.dma_start(out=words[t][:], in_=src[0].rearrange("p t i -> p (t i)").bitcast(I32))

        names = ("hi", "lo", "wi", "neg_wi")
        hi32 = keep.tile([P, PACK, N], F32, name="hi32")
        lo32 = keep.tile([P, PACK, N], F32, name="lo32")
        w16 = {w: keep.tile([P, N, PACK], BF16, name=w + "_bf16", tag=w, align_bytes=64) for w in names}
        w_codes = {w: keep.tile([P, N], U32, name=w + "_codes", align_bytes=64) for w in names}
        w_scales = {w: keep.tile([P, N], U8, name=w + "_scales", align_bytes=64) for w in names}
        wi_by_n = wi_raw[:].rearrange("p j n -> p n j")
        nc.vector.tensor_scalar(
            out=hi32[:].bitcast(I32),
            in0=wr_raw[:].bitcast(I32),
            scalar1=HI_MASK,
            scalar2=None,
            op0=ALU.bitwise_and,
        )
        nc.vector.tensor_tensor(out=lo32[:], in0=wr_raw[:], in1=hi32[:], op=ALU.subtract)
        nc.scalar.activation(w16["hi"][:], hi32[:].rearrange("p j n -> p n j"), ACT.Copy)
        nc.scalar.activation(w16["lo"][:], lo32[:].rearrange("p j n -> p n j"), ACT.Copy)
        nc.scalar.activation(w16["wi"][:], wi_by_n, ACT.Copy)
        nc.scalar.activation(w16["neg_wi"][:], wi_by_n, ACT.Copy, scale=-1.0)

        def quantise(w):
            nc.vector.quantize_mx(
                out=w_codes[w][:].bitcast(FP8X4),
                scales=w_scales[w][:],
                in_=w16[w][:].rearrange("p n j -> p (n j)"),
            )

        def gather(c, t):
            entries = offsets[:, c * CHUNK // GROUP : (c + 1) * CHUNK // GROUP]
            g_scales = ring.tile([P, CHUNK], U8, name="g_scales%d" % t, align_bytes=64)
            if t == 0:
                g_words = keep.tile([P, CHUNK], U32, name="g_words0", tag=names[c % WORD_SLOTS], align_bytes=64)
            else:
                g_words = ring.tile([P, CHUNK], U32, name="g_words1", bufs=WORD_SLOTS, align_bytes=64)
            nc.vector.tensor_copy(g_scales[:], scales[t][:].bitcast(U8).indirect(entries))
            nc.vector.tensor_copy(g_words[:], words[t][:].bitcast(U32).indirect(entries))
            return g_words, g_scales

        def mx_pass(acc, w, h, gathered, t, start, stop):
            cols = slice(h * P, (h + 1) * P)
            g_words, g_scales = gathered
            nc.tensor.matmul_mx(
                out=acc[:],
                lhsT=w_codes[w][:, cols].bitcast(FP8X4),
                lhsT_scale=w_scales[w][:, cols],
                rhs=g_words[:].bitcast(FP8X4),
                rhs_scale=g_scales[SCALE_ROW[t] : P, :],
                start=start,
                stop=stop,
            )

        def finish(h, pieces):
            for j0, width, total in pieces:
                result = work.tile([P, width], F32, name="result")
                nc.scalar.activation(result[:], total[:], ACT.Sqrt)
                nc.sync.dma_start(out=out[h * P : (h + 1) * P, j0 : j0 + width], in_=result[:])

        for w in names:
            quantise(w)
        pending = []
        for c in range(CHUNKS):
            v = gather(c, 0)
            v2 = gather(c, 1)
            zr = [psum.tile([P, CHUNK], F32, name="zr%d" % h) for h in range(HALVES)]
            zi = [psum.tile([P, CHUNK], F32, name="zi%d" % h) for h in range(HALVES)]
            last = c == CHUNKS - 1
            for h in range(HALVES):
                mx_pass(zr[h], "hi", h, v, 0, True, False)
            for h in range(HALVES):
                mx_pass(zr[h], "lo", h, v, 0, False, False)
            mx_pass(zi[0], "wi", 0, v, 0, True, False)
            if last:
                mx_pass(zi[1], "wi", 1, v, 0, True, False)
            mx_pass(zr[0], "neg_wi", 0, v2, 1, False, True)
            mx_pass(zi[0], "hi", 0, v2, 1, False, False)
            mx_pass(zi[0], "lo", 0, v2, 1, False, True)
            mx_pass(zr[1], "neg_wi", 1, v2, 1, False, True)
            mx_pass(zi[1], "hi", 1, v2, 1, not last, False)
            if not last:
                mx_pass(zi[1], "wi", 1, v, 0, False, False)
            mx_pass(zi[1], "lo", 1, v2, 1, False, True)
            for h in range(HALVES):
                zr_sq = work.tile([P, CHUNK], F32, name="zr_sq")
                zi_sq = work.tile([P, CHUNK], F32, name="zi_sq")
                nc.scalar.activation(zr_sq[:], zr[h][:], ACT.Square, bias=zero_bias[:])
                nc.scalar.activation(zi_sq[:], zi[h][:], ACT.Square, bias=zero_bias[:])
                very_last = last and h == HALVES - 1
                width = CHUNK // 2 if very_last else CHUNK
                pieces = []
                for j0 in range(0, CHUNK, width):
                    total = work.tile([P, width], F32, name="total")
                    adder = nc.vector if last else nc.gpsimd
                    adder.tensor_tensor(
                        out=total[:], in0=zr_sq[:, j0 : j0 + width], in1=zi_sq[:, j0 : j0 + width], op=ALU.add
                    )
                    pieces.append((c * CHUNK + j0, width, total))
                pending.append((h, pieces))
                if len(pending) > SQRT_LAG:
                    finish(*pending[-1 - SQRT_LAG])
        for late in pending[-SQRT_LAG:]:
            finish(*late)
